import numpy as np, ml_dtypes
CORES = [3,11,19,27,35,43,51,59]
N = 8
BF = ml_dtypes.bfloat16
def entries(a):
    return np.ascontiguousarray(a.T).reshape(-1)
def table(e):
    return np.ascontiguousarray(np.reshape(e, (-1, 16)).T).astype(np.int32)
def f(rng, *shape):
    return (rng.standard_normal(shape, dtype=np.float32) * np.exp2(rng.integers(-2, 3, shape[:-1] + (1,)))).astype(BF)
def wide(rng, *shape):
    v = f(rng, *shape).astype(np.float32); k = shape[:-2] + (1, shape[-1])
    return (v * np.exp2(rng.integers(-6, 7, k)) * (rng.random(k) > 0.0625)).astype(BF)
R, S1, S2, CAPP = 2048, 512, 1024, 32
T1, T2 = 0, 100
def orders(rng):
    return np.stack([rng.permutation(R) for r in range(N)])
def values(rng, order, n1, m, lo):
    v = rng.integers(-60, 1, (N, R))
    for r in range(N):
        v[r, order[r, :n1[r]]] = rng.integers(1, 5, n1[r]); v[r, order[r, :m[r]]] = rng.integers(lo[r], 256, m[r])
    x = f(rng, N, 16, R); x[:, 0] = v.astype(np.float32).astype(BF); return x
def some(rng, order, n1, m, *shape):
    top = np.array([m, n1, R])[rng.integers(0, 3, shape)]
    return order[(rng.random(shape) * top).astype(np.int64)]
def ghosts(rng, r, *shape):
    return R + ((r + 1 + rng.integers(0, N - 1, shape)) % N) * CAPP + rng.integers(0, CAPP, shape)
def draw(rng, order, n1, m, lo):
    x = values(rng, order, n1, m, lo); nb = []; bd = []
    for r in range(N):
        nb.append(np.where(rng.random((6, R)) < 0.7, some(rng, order[r], n1[r], m[r], 6, R), ghosts(rng, r, 6, R)))
        bd.append(table(some(rng, order[r], n1[r], m[r], N * CAPP)))
    return {"x": x, "nb": np.stack(nb).astype(np.int32), "bd": np.stack(bd)}
def setup_inputs(rng):
    return draw(rng, orders(rng), rng.integers(3 * S1 // 4, S1 + 1, N), np.full(N, S2 // 8), np.full(N, 40))
def setup_inputs_full(rng):
    order = orders(rng); a = int(rng.integers(0, N)); order[a] = np.arange(R); order[(a + 1) % N] = np.arange(R)[::-1]
    return draw(rng, order, np.full(N, S1), np.full(N, S2 // 8), np.full(N, 200))
def setup_inputs_ties(rng):
    order = orders(rng); n1 = rng.integers(3 * S1 // 4, S1 + 1, N); m = S2 // 8
    d = draw(rng, order, n1, np.full(N, m), np.full(N, 40)); x, nb = d["x"], d["nb"]; bd = []
    for r in range(N):
        h = order[r, :m]; c = order[r, n1[r]:]
        x[r, 0, h] = rng.integers(99, 102, m).astype(np.float32).astype(BF); x[r, 0, c] = rng.integers(-1, 1, len(c)).astype(np.float32).astype(BF)
        nb[r][:, h] = np.where(rng.random((6, m)) < 0.5, h[rng.integers(0, m, (6, m))], ghosts(rng, r, 6, m))
        nb[r][:, h[0]] = h[0]; x[r, 0, h[0]] = 100; nb[r][:, h[1]] = h[1]; x[r, 0, h[1]] = 101
        bd.append(table(h[rng.integers(0, m, N * CAPP)]))
    d["bd"] = np.stack(bd); return d
def setup_inputs_thin(rng):
    order = orders(rng); n1 = rng.integers(3 * S1 // 4, S1 + 1, N); m = np.minimum(S2 // 4, n1)
    d = draw(rng, order, n1, m, np.full(N, 40)); x, nb, bd = d["x"], d["nb"], d["bd"]; first = int(rng.integers(0, 6))
    for r in range(N):
        k = int(m[r]); h = order[r, :k]; c = order[r, n1[r]:]
        x[r, 0, h] = rng.integers(101, 104, k).astype(np.float32).astype(BF)
        nb[r][:, h] = np.where(rng.random((6, k)) < 0.5, h[rng.integers(0, k, (6, k))], ghosts(rng, r, 6, k))
        nb[r][(first + r) % 6, h] = c[rng.integers(0, len(c), k)]
        bd[r] = table(h[rng.integers(0, k, N * CAPP)])
    return d
def setup_inputs_far(rng):
    order = orders(rng); n1 = rng.integers(3 * S1 // 4, S1 + 1, N); m = np.full(N, S2 // 8); lo = np.full(N, 40); a = int(rng.integers(0, N)); b = (a + 1) % N; s = int(rng.integers(1, N))
    n1[a] = S1 // 8; m[a] = S2 // 64; lo[a] = 200
    d = draw(rng, order, n1, m, lo); nb, bd = d["nb"], d["bd"]
    for r in range(N):
        if r != a: nb[r] = R + ((r + s) % N) * CAPP + rng.integers(0, CAPP, (6, R))
        top = np.where(rng.random(N * CAPP) < 0.5, m[r], n1[r]); e = (rng.random(N * CAPP) * top).astype(np.int64)
        if r == a: e = rng.integers(n1[a], R, N * CAPP)
        if r == b: e = rng.integers(0, m[b], N * CAPP)
        bd[r] = table(order[r][e])
    return d
def setup_inputs_spread(rng):
    d = setup_inputs(rng); d["x"][:, 1:] = wide(rng, N, 16, R)[:, 1:]; return d
def grow(x, nb, bd):
    v = np.concatenate([a.astype(np.float64).T for a in x])
    w = np.stack([entries(a) for a in bd]).astype(np.int64).reshape(N, N, CAPP); near = []
    for r in range(N):
        ext = np.concatenate([r * R + np.arange(R), (R * np.arange(N)[:, None] + w[:, r]).reshape(-1)])
        near.append(ext[nb[r]].T)
    near = np.concatenate(near)
    p = np.flatnonzero(v[:, 0] > T1); number = np.full(N * R, -1); number[p] = np.arange(len(p)); kids = []
    for o in range(8):
        c = v[p].copy()
        for d in range(3): c += 0.125 * (v[near[p, 2 * d + (o >> d & 1)]] - v[p])
        kids.append(c)
    return v, near, p, number, np.stack(kids)
def check_inputs(d):
    bad = []; x = d["x"].astype(np.float32); nb, bd = d["nb"], d["bd"]
    if not np.isfinite(x).all() or not (np.abs(x) <= 65536).all(): bad.append("x finite and of size at most 65536")
    elif (x[:, 0] != np.floor(x[:, 0])).any() or (np.abs(x[:, 0]) > 256).any(): bad.append("x channel 0")
    own = (nb - R) // CAPP == np.arange(N)[:, None, None]
    if (nb < 0).any() or (nb >= R + N * CAPP).any() or own.any(): bad.append("nb")
    if (bd < 0).any() or (bd >= R).any(): bad.append("bd")
    if bad: return bad
    v, near, p, number, c1 = grow(d["x"], nb, bd); q = p // R
    if (np.bincount(q, minlength=N) > S1).any(): bad.append("splits of level 1")
    if (np.bincount(q[np.nonzero(c1[:, :, 0] > T2)[1]], minlength=N) > S2).any(): bad.append("splits of level 2")
    return bad
def reference(x, nb, bd):
    v, near, p, number, c1 = grow(x, nb, bd)
    O, S = np.nonzero(c1[:, :, 0] > T2)
    number2 = np.full(c1.shape[:2], -1); number2[O, S] = np.arange(len(O)); mid = c1[O, S]; val = {}; fine = {}
    for d in range(3):
        for b in range(2):
            m = near[p[S], 2 * d + b]; t = np.where((O >> d & 1) != b, S, number[m]); o = O ^ (1 << d)
            val[d, b] = np.where((t >= 0)[:, None], c1[o, t], v[m]); fine[d, b] = np.where(t >= 0, number2[o, t], -1)
    c2 = []
    for o in range(8):
        c = mid.copy()
        for d in range(3): c += 0.125 * (val[d, o >> d & 1] - mid)
        c2.append(c)
    c2 = np.stack(c2); z = 0.25 * c2
    for o in range(8):
        for d in range(3):
            b = o >> d & 1; other = c2[o ^ (1 << d)]; u = fine[d, b]
            z[o] += 0.125 * (other + np.where((u >= 0)[:, None], other[u], val[d, b]))
    y1 = np.zeros((N, 8, 16, S1)); y2 = np.zeros((N, 8, 16, S2))
    for r in range(N):
        a = c1[:, p // R == r]; y1[r, :, :, :a.shape[1]] = a.transpose(0, 2, 1)
        a = z[:, p[S] // R == r]; y2[r, :, :, :a.shape[1]] = a.transpose(0, 2, 1)
    return {"y1": y1.reshape(N, 128, S1).astype(np.float32), "y2": y2.reshape(N, 128, S2).astype(np.float32)}

from concourse.bass import DstId, RemoteDMATransfer
from concourse.mybir import dt, AluOpType, AxisListType, ActivationFunctionType

F32, BF, F16, I32, U16 = "float32", "bfloat16", "float16", "int32", "uint16"
SB = "sbuf"
SCRATCH = {"ps": ("psum", [128, 4096], F32)}
for _d, _l in ((BF, "xraw 2048 x0 16 XB 3328 PA 256 PB 256 I16b 128 M1b 128 M1o 1024 WB 288 FA 1024"),
               (I32, "bdi 16 nbraw 256 IC 16 ci 32"), (U16, "ul 512"),
               (F16, "Idh 128 RTo 128 RTi 128 WH 432 Sg 512 Sel 512 vh 16 R4 512 H1 512 Igc 512 Db 256 Dc 256"),
               (F32, "TB 11264 AT 2816 PO 1024 LO 1024 cc 64 MG 1024 HG 1024 WF 144 sm 1024 ios 256 Fd 256 W1 1280 F2 512 W2 2560 "
                     "Y1 512 AA 1024 C2 1024 G0 1024 G1 1024 G2 1024 Y2 1024 PM 128 CM 128 GM 128 FB 128 I16f 128 TRI 128 BO 128 LG 128 "
                     "TU 128 BI 128 EQ 128 EQI 128 NE 128 M1f 128 MB 128 S6 128 Pa 128 Pb 128 E8 128 t0 128 t1 128 t2 128 t3 128 t4 128 "
                     "t5 128 t6 128")):
    _l = _l.split()
    for _i in range(0, len(_l), 2):
        SCRATCH[_l[_i]] = (SB, [128, int(_l[_i + 1])], _d)
NDMA = 24
SEMAPHORES = ["qV", "qA", "qP", "qG", "arrA", "arrB", "arrC", "sent"] + ["d%d" % i for i in range(NDMA)]

OP = AluOpType
AF = ActivationFunctionType
V0 = 1024
XO, CG = 6144, 8192
ORDER = [1,0,2,10,25,18,19,20,35,11,37,34,36,24,23,41,21,3,38,44,43,4,58,56,6,54,59,12,107,55,100,8,101,13,60,106,53,14,39,48,26,15,27,62,40,16,130,47,153,135,133,139,137,155,136,156,7,9,5,131,157,134,17,138,99,140,132,67,158,46,154,141,105,61,160,159,45,162,164,111,161,51,49,52,42,64,163,50,98,69,142,165,175,144,170,166,172,168,68,176,115,63,177,178,96,174,179,84,109,102,74,82,66,112,80,108,151,78,88,167,113,171,57,122,114,145,123,169,180,143,181,173,110,86,116,117,118,182,183,124,120,94,146,184,119,185,186,187,188,197,70,189,147,76,148,196,72,236,218,22,199,190,121,95,198,125,103,219,240,220,221,234,200,191,238,202,237,201,241,235,104,192,239,222,127,193,223,126,129,128,97,150,203,152,204,242,244,224,205,194,248,225,206,29,226,195,250,246,245,243,249,207,227,81,247,149,266,260,262,264,228,229,208,267,263,209,261,265,268,28,230,231,278,210,232,32,276,233,33,31,258,259,30,269,211,212,213,71,251,65,75,277,214,83,215,85,91,77,284,89,90,281,295,301,299,297,279,282,253,285,216,217,254,92,270,283,280,87,272,286,79,287,273,274,288,298,255,289,256,257,93,290,271,300,291,307,275,309,305,73,308,310,293,306,303,294,292,304,296,302,327,328,312,320,336,329,252,311,315,313,319,323,335,331,339,314,330,316,321,322,337,332,338,324,340,318,317,326,334,325,333,342,341]


def rank_program(g, core, T, topo):
    rank = T.rank_of(core)
    if rank is None:
        return
    n = len(T.cores)
    Q = {"V": g.vector, "A": g.scalar, "P": g.tensor, "G": g, "S": g.sync}
    nodes = []
    log = {}

    def norm(a):
        return (a[0], a[1], a[2], a[3] if len(a) > 3 else 1, a[4] if len(a) > 4 else 0, a[5] if len(a) > 4 else 128)

    def reg(a):
        nm, lo, hi, st, p0, p1 = norm(a)
        return T[nm][p0:p1, lo:hi:st] if st != 1 else T[nm][p0:p1, lo:hi]

    def node(e, kind, fn, R, W, after=()):
        dep = {a: True for a in after}
        for (regs, wr) in ((R, False), (W, True)):
            for r in regs:
                nm, lo, hi, st, p0, p1 = norm(r)
                for (a, b, s2, q0, q1, w2, k) in log.get(nm, ()):
                    e2 = nodes[k]["e"]
                    if nm == "ps" and (e2 != e or e == "P"):
                        if a // 512 > (hi - 1) // 512 or (b - 1) // 512 < lo // 512:
                            continue
                    elif a >= hi or b <= lo or q0 >= p1 or q1 <= p0 or (st == s2 and (a - lo) % st) or not (wr or w2):
                        continue
                    dep[k] = not (e == "P" and e2 == "P")
        nodes.append({"e": e, "kind": kind, "fn": fn, "dep": dep, "p0": norm(W[0])[4] if W else 0})
        for (regs, wr) in ((R, False), (W, True)):
            for r in regs:
                nm, lo, hi, st, p0, p1 = norm(r)
                log.setdefault(nm, []).append((lo, hi, st, p0, p1, wr, len(nodes) - 1))
        return len(nodes) - 1

    def dma(e, out, in_, R, W):
        node(e, "dma", lambda: Q[e].dma_start(out, in_), R, W)

    def istup(x):
        return isinstance(x, tuple)

    def val(x):
        return reg(x) if istup(x) else x

    def src(a):
        if istup(a[0]):
            return reg(a[0]).indirect(reg(a[1])), [a[0], a[1]]
        return reg(a), [a]

    def ts(out, a, s1, o0, s2=None, o1=None):
        ap, R = src(a)
        R = R + [s for s in (s1, s2) if istup(s)]
        if o1 is None:
            node("V", "op", lambda: g.vector.tensor_scalar(reg(out), ap, val(s1), None, o0), R, [out])
        else:
            node("V", "op", lambda: g.vector.tensor_scalar(reg(out), ap, val(s1), val(s2), o0, o1), R, [out])

    def tt(out, a, b, o):
        ap, R = src(a)
        node("V", "op", lambda: g.vector.tensor_tensor(reg(out), ap, reg(b), o), R + [b], [out])

    def cp(out, a):
        ap, R = src(a)
        node("V", "op", lambda: g.vector.tensor_copy(reg(out), ap), R, [out])

    def scat(win, lst, a):
        node("V", "op", lambda: g.vector.tensor_copy(reg(win).indirect(reg(lst)), reg(a)), [a, lst], [win])

    def scan(out, a, z):
        node("V", "op", lambda: g.vector.tensor_tensor_scan(reg(out), reg(a), reg(z), 0.0, OP.add, OP.add), [a, z], [out])

    def ms(out, c):
        node("V", "op", lambda: g.vector.memset(reg(out), c), [], [out])

    def act(out, a, scale=1.0, bias=0.0, f=AF.Identity):
        ap, R = src(a)
        R = R + [s for s in (scale, bias) if istup(s)]
        node("A", "op", lambda: g.scalar.activation(reg(out), ap, f, bias=val(bias), scale=val(scale)), R, [out])

    def mms(calls):
        def fn():
            r = None
            for i, (o, l, x, s, t) in enumerate(calls):
                if i and norm(l)[4] != norm(calls[i - 1][1])[4]:
                    cnt["P"] += 1
                    r.then_inc(T.sem.qP, 1)
                    wait("P", "qP", cnt["P"])
                r = g.tensor.matmul(reg(o), reg(l), reg(x), s, t)
            return r
        node("P", "op", fn, [x[1] for x in calls] + [x[2] for x in calls], [x[0] for x in calls])

    def mm(out, l, r, start=True, stop=True):
        mms([(out, l, r, start, stop)])

    def iota(out, pat, base, cm, small=True):
        if small:
            node("G", "op", lambda: g.iota(reg(out), pat, base, cm, allow_small_or_imprecise_dtypes=True), [], [out])
        else:
            node("G", "op", lambda: g.iota(reg(out), pat, base, cm), [], [out])

    def asel(out, a, pat, base, cm):
        node("G", "op", lambda: g.affine_select(reg(out), reg(a), pat, OP.is_equal, 0.0, base, cm), [a], [out])

    def diag(out, w, w0, a, a0, k, m=16):
        st = 16 // m
        calls = [(out, (w, w0 + (m - 1 - r) * st, w0 + (m - 1 - r) * st + 128), (a, a0 + r, a0 + m * k, m), r == 0, r == m - 1) for r in range(m)]
        for i in range(0, m, 4):
            mms(calls[i:i + 4])

    def others(w, l0=0):
        return [(lo, hi) for (lo, hi) in ((l0, l0 + rank * w), (l0 + (rank + 1) * w, l0 + n * w)) if hi > lo]

    def exchange(pay, w, land, l0, arr):
        trs = []
        for q in range(n):
            if q == rank:
                continue
            dst = T.cores[q]
            rid, pid, se = topo.addr(dst)
            trs.append(RemoteDMATransfer(dst_ids=[DstId(rid=rid, pnc=pid)], dma_engine_mask=1 << topo.engines(core, dst)[len(trs)],
                                         remote_sem=T.sem[arr], src=T[pay][:, q * w:(q + 1) * w],
                                         dst=T[land][:, l0 + rank * w:l0 + (rank + 1) * w]))
        k = node("G", "rem", lambda: g.remote_dma_fused(trs, local_sem=T.sem.sent), [(pay, lo, hi) for (lo, hi) in others(w)], [])
        node("R", arr, None, [], [(land, lo, hi) for (lo, hi) in others(w, l0)], [k])

    def col(i, p0=0, p1=128):
        return ("cc", i, i + 1, 1, p0, p1)

    def M(nm, p0=0, p1=128):
        return (nm, 0, 128, 1, p0, p1)

    def s8(nm, k=8):
        return (nm, 0, 16 * k, 16)

    def one(c, p1=128):
        return ("I16f", c, c + 1, 1, 0, p1)

    def tb(lo, hi):
        return ("TB", V0 + lo, V0 + hi)

    def bank(b, lo=0, hi=512):
        return ("ps", 512 * b + lo, 512 * b + hi)

    ZX = 2048 + 32 * rank
    ZC = 4096 + 32 * rank
    cC, cJ, cB, cA, cFa, cFb, cW, cLo, cHi, cOff, cWc, cW1, cPw, cJx, cSl, cSh, cAl, cGa, cT = range(19)
    lBD, lSP, lD1, lB, lB1, lO, lD2, lA, lS, lG = (0, 16), (16, 32), (32, 48), (48, 80), (80, 96), (96, 160), (160, 192), (192, 256), (256, 320), (320, 512)

    def ul(x, lo=0, hi=None):
        return ("ul", x[0] + lo, x[1] if hi is None else x[0] + hi)

    sm_at = [0]

    def sm(k):
        sm_at[0] += k
        return ("sm", sm_at[0] - k, sm_at[0])

    def sub(a, lo, hi):
        return (a[0], a[1] + lo, a[1] + hi)

    dma("S", T.xraw[0:16, :], T.x[:, :], [], [("xraw", 0, 2048)])
    dma("A", T.bdi[0:16, :], T.bd[:, :], [], [("bdi", 0, 16)])
    dma("S", T.x0[:, :], T.x[0, :], [], [("x0", 0, 16)])
    iota(("nbraw", 0, 256), [[1, 256]], -96, 16, False)
    for c in range(6):
        dma("A" if c % 2 == 0 else "S", T.nbraw[c:128:16, :], T.nb[c, :], [("nbraw", 0, 256)], [("nb%d" % c, 0, 1)])

    iota(("IC", 0, 16), [[1, 16]], 0, 16, False)
    iota(M("CM"), [[0, 8], [1, 16]], 0, 0)
    iota(M("PM"), [[-1, 128]], 0, 1)
    iota(M("GM"), [[1, 8], [0, 16]], 0, 0)
    iota(M("FB", 0, 32), [[0, 4], [1, 2], [0, 16]], 0, 0)
    iota(M("FB", 32, 64), [[0, 2], [1, 2], [0, 32]], 0, 0)
    iota(M("FB", 64, 96), [[1, 2], [0, 64]], 0, 0)
    iota(("ios", 0, 256), [[1, 256]], 0, 0)
    ms(M("FB", 96, 128), 0.0)
    ms(("W1", 0, 256), 0.0)
    ms(("W1", 256, 512), 0.0)
    ms(("XB", ZX, ZX + 32), 0.0)
    ms(("XB", 768 + ZX, 768 + ZX + 32), 0.0)
    ms(("WB", 0, 288), 0.0)
    ms(("WF", 0, 144), 0.0)
    ms(col(cA, 0, 96), 0.125)
    ms(col(cA, 96, 128), 0.625)
    ms(M("E8"), 0.125)
    ms(col(cAl, 0, 64), 3 / 64)
    ms(col(cAl, 64, 96), -3 / 64)
    ms(col(cAl, 96, 128), 25 / 64)
    ms(col(cGa, 0, 64), 1 / 64)
    ms(col(cGa, 64, 96), 4 / 64)
    ms(col(cGa, 96, 128), 0.0)
    ts(("ci", 0, 1), ("IC", 0, 1), 4, OP.arith_shift_right, 15, OP.bitwise_and)
    ts(("ci", 1, 2), ("IC", 0, 1), 8, OP.arith_shift_right)
    ts(("ci", 2, 3), ("IC", 0, 1), 8, OP.arith_shift_right, 1, OP.bitwise_and)
    ts(("ci", 16, 32), ("IC", 0, 16), 255, OP.bitwise_and)
    for k in range(3):
        ts(("WH", 144 * k, 144 * k + 144), ("W1", 0, 144), 0.0, OP.mult)
    cp(("cc", 0, 3), ("ci", 0, 3))
    cp(ul(lSP), ("ci", 16, 32))
    ts(M("I16b"), M("CM"), col(cC), OP.is_equal)
    ts(M("I16f"), M("CM"), col(cC), OP.is_equal)
    dump1, cellm, w3, ct, uio, dump2, um, row, tmp = sm(16), sm(16), sm(8), sm(8), sm(64), sm(32), sm(64), sm(8), sm(8)
    ts(dump1, ("ci", 16, 32), -1536.0, OP.add)
    ts(cellm, ("IC", 0, 16), -1536.0, OP.add)
    ts(M("TRI"), M("PM"), 0.0, OP.is_lt)
    ts(M("Idh"), M("PM"), 0.0, OP.is_equal)
    for a in range(4):
        ts(("Sel", 128 * a, 128 * a + 128, 1, 0, 4), M("Idh", 0, 4), 0.0, OP.mult, one(a, 4), OP.add)
    act(col(cFa), one(7), -1.0, 1.0)
    act(col(cFb), one(7), 1153.0, -1152.0)
    act(col(cW), one(7), float(1152 - ZX))
    act(col(cLo), one(0), -4000.0)
    act(col(cHi), one(0), 4000.0, 1.0)
    act(col(cT), col(cC), -256.0, -511.0)
    act(col(cOff), one(0), 511.0, col(cT))
    act(col(cT + 1), col(cOff), 1.0, 1280.0)
    ts(w3, s8("GM"), 6.0, OP.min, col(cC), OP.is_equal)
    ts(M("BO"), M("GM"), col(cJ), OP.is_equal)
    ts(("WH", 15, 143, 16), w3, col(cW), OP.add)
    ts(("WH", 144 + 15, 144 + 143, 16), s8("BO"), one(0), OP.mult)
    act(("WB", 144 + 15, 144 + 143, 16), s8("BO"), one(0))
    act(("WF", 15, 143, 16), w3)
    ts(M("EQ"), M("FB"), col(cB), OP.is_equal)
    tt(M("EQI"), M("EQ"), M("I16f"), OP.mult)
    act(ct, s8("EQ"), col(cA))
    act(M("M1b"), M("EQI"), col(cA))
    act(M("M1f"), M("EQI"), col(cA))
    for o in range(8):
        act(("M1o", 128 * o, 128 * o + 128), M("I16f"), sub(ct, o, o + 1))
        act(("MG", 128 * o, 128 * o + 128, 1, 0, 96), M("EQI", 0, 96), ("EQ", 16 * o, 16 * o + 1, 1, 0, 96))
    act(("WB", 15, 143, 16), ct, one(0))
    act(M("S6"), M("I16f"), ("BO", 96, 97))
    act(M("t5"), M("EQI"), col(cAl))
    act(M("t6"), M("I16f"), col(cGa))
    tt(M("MB"), M("t5"), M("t6"), OP.add)
    tt(M("NE"), M("I16f"), M("EQI"), OP.subtract)
    ts(M("t0"), M("PM"), 0.0, OP.is_ge, -1.0, OP.mult)
    ts(M("LG"), M("GM"), col(cJ), OP.is_gt)
    ts(M("BI"), M("PM"), 0.0, OP.is_equal, -2048.0, OP.mult)
    tt(M("TU"), M("t0"), M("BO"), OP.mult)
    act(uio, ("ios", 0, 64), 16.0, col(cC))
    act(row, s8("GM"), -0.5, 1.75)
    act(col(cT + 2), one(2), 1.0, one(3))
    act(col(cJx), col(cB), -2.0, col(cJ))
    act(col(cT + 3), col(cJx), 1.0, 1.0)
    act(dump2, sub(uio, 0, 32), 1.0, -1024.0)
    act(um, uio, 1.0, float(-ZC - 1024))
    tt(tmp, s8("EQ"), row, OP.mult)
    act(col(cWc), col(cT + 2), 1792.0, one(0))
    act(col(cW1), one(1), 256.0)
    act(col(cSl), one(0), 768.0, one(1))
    act(col(cT + 4), one(0), 256.0, one(2))
    act(col(cSh), col(cSl), 1.0, col(cT + 4))
    node("V", "op", lambda: g.vector.tensor_reduce(reg(col(cPw)), reg(tmp), AxisListType.X, OP.add), [tmp], [col(cPw)])
    act(col(cT + 5), col(cPw), 1.0, -33.0)
    act(col(cT + 6), col(cT + 5), col(cW1), col(cWc))
    act(M("t1"), M("GM"), col(cW1), col(cT + 6))
    ts(M("t3"), M("CM"), col(cJ), OP.is_equal)
    ts(M("t4"), M("CM"), col(cT + 3), OP.is_equal)
    tt(M("t2"), M("t1"), M("EQ"), OP.mult)
    ts(("Sg", 0, 256), ("ios", 0, 256), one(0), OP.mult, col(cSl), OP.add)
    ts(("Sg", 256, 512), ("ios", 0, 256), one(0), OP.mult, col(cSh), OP.add)
    tt(M("RTo"), M("t2"), M("t3"), OP.mult)
    tt(M("RTi"), M("t2"), M("t4"), OP.mult)
    a1, a2, a4 = sm(4), sm(4), sm(4)
    act(col(cT + 7), col(cPw), 1.0, -26.0)
    act(a1, sub(tmp, 0, 4), -4.0, col(cT + 7))
    tt(a2, a1, s8("GM", 4), OP.subtract)
    act(a4, a2, col(cW1), col(cWc))
    for b in range(4):
        ts(("WH", 288 + 12 + b, 288 + 140, 16), s8("BO"), sub(a4, b, b + 1), OP.mult)

    bdf = sm(16)
    cp(bdf + (1, 0, 16), ("bdi", 0, 16, 1, 0, 16))
    mm(bank(4, 0, 16), M("I16f", 0, 16), bdf + (1, 0, 16))
    cp(ul(lBD), bank(4, 0, 16))
    for b in range(4):
        mm(bank(b), M("I16b", 0, 16), ("xraw", 512 * b, 512 * b + 512, 1, 0, 16))
        (act if b % 2 == 0 else cp)(("XB", 512 * b, 512 * b + 512), bank(b))
    act(("PA", 0, 256), (("XB", 0, 2048), ul(lBD)))
    exchange("PA", 32, "XB", 2048, "arrA")
    iota(("W2", 0, 512), [[0, 512]], 0, 0)
    iota(("W2", 512, 1024), [[0, 512]], 0, 0)
    asel(M("Pb"), M("E8"), [[64, 2], [32, 2], [-1, 32]], -96, 1)
    asel(("Pa", 0, 64), ("E8", 0, 64), [[-32, 2], [16, 2], [-1, 16]], -80, 1)
    asel(("Pa", 64, 128), ("E8", 0, 64), [[-32, 2], [16, 2], [-1, 16]], -16, 1)
    for b in range(4):
        (act if b % 2 == 0 else cp)(tb(XO + 512 * b, XO + 512 * b + 512), ("XB", 512 * b, 512 * b + 512))

    fl, flm, flp, sc, u1, u2, u3, u4 = [sm(16) for i in range(8)]
    ts(fl, ("x0", 0, 16), 0.0, OP.is_gt)
    ts(flm, ("x0", 0, 16), 0.0, OP.is_gt, -2049.0, OP.mult)
    ts(flp, ("x0", 0, 16), 0.0, OP.is_gt, 4095.0, OP.mult)
    scan(sc, fl, ("W1", 0, 16))
    mm(bank(5, 0, 1), M("TRI"), sub(sc, 15, 16))
    tt(u3, sc, flp, OP.add)
    tt(u1, sc, flm, OP.add)
    ts(u4, u3, bank(5, 0, 1), OP.add, -3328.0, OP.add)
    tt(u2, u1, dump1, OP.min)
    tt(("vh", 0, 16), u4, cellm, OP.max)
    ts(ul(lD1), u2, bank(5, 0, 1), OP.add, 2048.0, OP.add)
    mms([(("ps", 3072 + 16 * r, 3072 + 16 * r + 16, 1, 0, 4), ("Idh", r, 128, 32), ("vh", 0, 16), True, True) for r in range(32)])
    cp(("R4", 0, 512, 1, 0, 4), ("ps", 3072, 3584, 1, 0, 4))
    for a in range(4):
        mm(bank(a), ("Sel", 128 * a, 128 * a + 128, 1, 0, 4), ("R4", 0, 512, 1, 0, 4))
        act(("AT", 512 * a, 512 * a + 512), bank(a), 1.0, col(cOff))
    act(("AT", 2048, 2304), ("ios", 0, 256), 1.0, col(cT + 1))
    node("V", "op", lambda: g.vector.tensor_scalar(T.Fd[:, :], T.nbraw[:, :].indirect(reg(ul(lSP))), reg(col(cFa)), reg(col(cFb)), OP.mult, OP.add),
         [("nb%d" % c, 0, 1) for c in range(6)] + [("nbraw", 0, 256), ul(lSP), col(cFa), col(cFb)], [("Fd", 0, 256)])
    scat(("W1", 0, 1280), ul(lD1), ("Fd", 0, 256))
    cp(("H1", 0, 512), ("W1", 0, 512))
    diag(bank(4, 0, 32), "WH", 0, "H1", 0, 32)
    ts(ul(lB), bank(4, 0, 32), float(ZX), OP.add)
    cp(("Db", 0, 256), (("AT", 0, 2048), ul(lBD)))
    diag(bank(7, 0, 16), "WH", 144, "Db", 0, 16)
    ts(ul(lB1), bank(7, 0, 16), 1536.0, OP.add)
    act(("AT", 2304, 2816), (("AT", 0, 2304), ul(lB)))
    ts(("Igc", 0, 512), ("AT", 2304, 2816), col(cLo), OP.max, col(cHi), OP.min)
    mms([(bank(5), M("RTo"), ("Igc", 0, 512), True, False), (bank(5), M("RTi"), ("Sg", 0, 512), False, True)])
    act(("F2", 0, 512), bank(5), 1.0, float(1536 + XO - ZC))
    ts(("Dc", 0, 256), (("AT", 0, 2816), ul(lB1)), col(cLo), OP.max, col(cHi), OP.min)
    diag(bank(7, 0, 64), "WH", 288, "Dc", 0, 64, 4)
    ts(ul(lO), bank(7, 0, 64), float(1536 + XO), OP.add)

    act(("XB", 2304, 2560), (("XB", 0, 2304), ul(lB, 0, 16)))
    cp(("XB", 2560, 2816), (("XB", 0, 2304), ul(lB, 16, 32)))
    act(("PB", 0, 128), (("XB", 0, 2816), ul(lB1, 0, 8)))
    cp(("PB", 128, 256), (("XB", 0, 2816), ul(lB1, 8, 16)))
    exchange("PB", 32, "XB", 2816, "arrB")
    for o in range(8):
        sg = [1 - 2 * (o >> d & 1) for d in range(3)]
        pc = (o & 1) + (o >> 1 & 1) + (o >> 2)
        for h in range(2):
            iota(("HG", 128 * o + 64 * h, 128 * o + 64 * h + 64, 1, 96, 128), [[sg[1], 2], [sg[0], 2], [0, 16]], 4 + pc + sg[2] * h, 0)

    def level1(blk, engs):
        for j in range(4):
            mms([(bank(j, 256 * h, 256 * h + 256), ("M1o", 128 * (2 * j + h), 128 * (2 * j + h) + 128), ("XB", 2304 + 256 * blk, 2560 + 256 * blk), True, True) for h in range(2)])
            (act if engs[j] == "A" else cp)(tb(2048 * blk + 512 * j, 2048 * blk + 512 * j + 512), bank(j))

    f2, sc2, v1, laf = sm(32), sm(32), sm(32), sm(64)
    diag(bank(4, 0, 32), "WB", 0, "XB", 2304, 32)
    ts(f2, bank(4, 0, 32), 100.0, OP.is_gt)
    scan(sc2, f2, ("W2", 0, 32))
    mms([(bank(5, 0, 32), M("BO"), sc2, True, False), (bank(5, 0, 32), M("TU"), f2, False, False), (bank(5, 0, 32), M("BI"), f2, False, True),
         (bank(5, 32, 33), M("LG"), sub(sc2, 31, 32), True, True)])
    tt(v1, bank(5, 0, 32), dump2, OP.min)
    ts(ul(lD2), v1, bank(5, 32, 33), OP.add, 2048.0, OP.add)
    scat(("W2", 0, 2560), ul(lD2), ("F2", 0, 512))
    diag(bank(6, 0, 64), "WF", 0, "W2", 0, 64)
    ts(ul(lA), bank(6, 0, 64), float(ZC), OP.add)
    ts(laf, bank(6, 0, 64), float(ZC), OP.add)
    level1(0, "AAAA")
    level1(1, "AAAA")
    mm(bank(4), M("M1b"), ("XB", 2304, 2816))
    act(("Y1", 0, 512), bank(4))
    dma("G", T.y1[:, :], T.Y1[:, :], [("Y1", 0, 512)], [])
    b1, b2, b3, gm_, lm, b4, b5 = [sm(64) for i in range(7)]
    mm(bank(7, 0, 64), M("S6"), laf)
    ts(b1, bank(7, 0, 64), 4096.0, OP.is_ge)
    tt(b2, b1, um, OP.mult)
    tt(b3, bank(7, 0, 64), b2, OP.add)
    ts(ul(lS), b3, 1024.0, OP.add)
    ts(gm_, laf, 4096.0, OP.is_ge, 2048.0, OP.mult)
    tt(lm, laf, gm_, OP.add)

    level1(2, "VAVA")
    cut = 28 + 8 * (rank < n // 2)
    for (e, c0, c1) in (("V", 0, cut), ("A", cut, 64)):
        rs = [(max(lo, c0), min(hi, c1)) for (lo, hi) in others(8) if min(hi, c1) > max(lo, c0)]

        def pick(e=e, rs=rs):
            r = []
            for (a, b) in rs:
                ap = reg(tb(0, CG)).indirect(reg(ul(lO, a, b)))
                r.append(g.vector.tensor_copy(T.PO[:, 16 * a:16 * b], ap) if e == "V" else g.scalar.activation(T.PO[:, 16 * a:16 * b], ap, AF.Identity))
            return r[-1]
        node(e, "op", pick, [tb(0, CG), ul(lO)], [("PO", 16 * a, 16 * b) for (a, b) in rs])
    exchange("PO", 128, "LO", 0, "arrC")
    for h in range(4):
        asel(("MG", 256 * h, 256 * h + 256, 1, 96, 128), ("HG", 256 * h, 256 * h + 256, 1, 96, 128), [[0, 16], [1, 16]], 16 * (h // 2), -1)

    cp(("AA", 0, 512), (tb(0, CG), ul(lA, 0, 32)))
    act(("AA", 512, 1024), (tb(0, CG), ul(lA, 32, 64)))
    cp(("XB", 3072, 3328), ("XB", 2816, 3072))
    for h in range(2):
        mm(bank(4 + h), M("M1f"), ("AA", 512 * h, 512 * h + 512))
        act(("C2", 512 * h, 512 * h + 512), bank(4 + h))
        act(("FA", 512 * h, 512 * h + 512), ("AA", 512 * h, 512 * h + 512), 1.0, -100.0625, AF.Sign)
    diag(bank(6, 0, 64), "WB", 144, "FA", 0, 64)
    tt(b4, bank(6, 0, 64), gm_, OP.mult)
    tt(b5, b4, lm, OP.add)
    mms([(bank(7, 64 * d, 64 * d + 64), M("NE", 32 * d, 32 * d + 32), b5 + (1, 32 * d, 32 * d + 32), True, True) for d in range(3)])
    cp(ul(lG), bank(7, 0, 192))
    for h in range(2):
        scat(("TB", 0, V0 + 4096), ul(lS, 32 * h, 32 * h + 32), ("C2", 512 * h, 512 * h + 512))
    for j in range(4):
        mm(bank(j), M("M1b"), ("XB", 2816, 3328), True, False)
        mm(bank(4 + j, 0, 256), M("MB"), ("AA", 256 * j, 256 * j + 256), True, False)

    for j in range(4):
        calls = []
        for h in range(2):
            o = 2 * j + h
            for (lo, hi) in others(32):
                calls.append((bank(j, 256 * h + lo, 256 * h + hi), ("MG", 128 * o, 128 * o + 128), ("LO", 4 * lo + min(o, 7 - o), 4 * hi, 4), False, False))
        calls[-1] = calls[-1][:4] + (True,)
        mms(calls)
        act(tb(CG + 512 * j, CG + 512 * j + 512), bank(j), 0.125)
    win = tb(0, CG + 2048)
    for h in range(4):
        lo, hi = 256 * h, 256 * h + 256
        act(("G0", lo, hi), (win, ul(lG, 16 * h, 16 * h + 16)))
        cp(("G1", lo, hi), (win, ul(lG, 64 + 16 * h, 80 + 16 * h)))
        mm(bank(4 + h, 0, 256), M("Pa"), ("G0", lo, hi), False, False)
        mm(bank(4 + h, 0, 256), M("Pb"), ("G1", lo, hi), False, True)
        act(("G2", lo, hi), (win, ul(lG, 128 + 16 * h, 144 + 16 * h)), 0.125)
        tt(("Y2", lo, hi), bank(4 + h, 0, 256), ("G2", lo, hi), OP.add)
        dma("S", T.y2[0:64, lo:hi], T.Y2[64:128, lo:hi], [("Y2", lo, hi)], [])
        dma("GGSA"[h], T.y2[64:128, lo:hi], T.Y2[0:64, lo:hi], [("Y2", lo, hi)], [])

    cnt = {e: 0 for e in "VAPG"}
    sig = {}
    gp0 = [0]
    waited = {}
    total = {}

    def wait(e, sem, v):
        if waited.get((e, sem), 0) < v:
            Q[e].wait_ge(T.sem[sem], v)
            waited[(e, sem)] = v

    for k in ORDER:
        nd = nodes[k]
        e = nd["e"]
        if e == "R":
            sig[k] = (nd["kind"], n - 1)
            total[nd["kind"]] = n - 1
            continue
        need = {}
        for d in nd["dep"]:
            if nd["dep"][d]:
                need[sig[d][0]] = max(need.get(sig[d][0], 0), sig[d][1])
        for sem in need:
            wait(e, sem, need[sem])
        if e == "G" and nd["kind"] == "op":
            if nd["p0"] != gp0[0]:
                wait(e, "qG", cnt[e])
            gp0[0] = nd["p0"]
        ins = nd["fn"]()
        if nd["kind"] == "rem":
            total["sent"] = total.get("sent", 0) + n - 1
        elif nd["kind"] == "dma":
            sem = "d%d" % len([s for s in total if s[0] == "d"])
            ins.then_inc(T.sem[sem], 16)
            total[sem] = 16
            sig[k] = (sem, 16)
        else:
            cnt[e] += 1
            ins.then_inc(T.sem["q" + e], 1)
            total["q" + e] = cnt[e]
            sig[k] = ("q" + e, cnt[e])
    for sem in total:
        if max([waited.get((e, sem), 0) for e in Q]) < total[sem]:
            wait("G", sem, total[sem])
